import numpy as np
import ml_dtypes


def mxq(x, axis, fmt="e4m3"):
    dtype, down = {"e4m3": (ml_dtypes.float8_e4m3fn, 7), "e5m2": (ml_dtypes.float8_e5m2, 14)}[fmt]
    v = np.moveaxis(np.asarray(x, np.float32).astype(ml_dtypes.bfloat16).astype(np.float64), axis, -1)
    blocks = v.reshape(v.shape[:-1] + (-1, 32))
    amax = np.abs(blocks).max(-1, keepdims=True)
    byte = np.maximum(np.where(amax > 0, np.frexp(amax)[1] - 1 + 127, 0) - down, 1)
    scale = np.exp2(byte - 127.0)
    codes = (blocks / scale).astype(np.float32).astype(dtype).astype(np.float64)
    return np.moveaxis((codes * scale).reshape(v.shape), -1, axis)


WIDE = False


def mx_kscale(k):
    if not WIDE:
        return np.ones(k)
    levels = np.array([10, -10, 5, -5, 0])
    if k % 512:
        return np.exp2(np.random.permutation(np.resize(levels, k // 32))).repeat(32)
    a = np.empty((k // 512, 16))
    for p in range(k // 512):
        a[p, :8] = np.random.permutation(np.resize(levels, 8))
        for g in range(8):
            far = levels[np.abs(levels - a[p, g]) >= 10]
            a[p, g + 8] = far[np.random.randint(len(far))]
    return np.exp2(a.ravel()).repeat(32)


def f64(x):
    return np.asarray(x).astype(np.float64)


def striped(idx):
    return np.tile(np.asarray(idx).reshape(-1, 16).T, (8, 1)).astype(np.uint16)


def unstriped(offs):
    return offs[:16].T.reshape(-1).astype(np.int64)


E2M1 = np.array([0.0, 0.5, 1.0, 1.5, 2.0, 3.0, 4.0, 6.0, -0.0, -0.5, -1.0, -1.5, -2.0, -3.0, -4.0, -6.0])


def pack_weight(w, fmt):
    k, n = w.shape
    w = f64(np.asarray(w, np.float32).astype(ml_dtypes.bfloat16)).reshape(k // 32, 32, n)
    amax = np.abs(w).max(1)
    if fmt == "e4m3":
        byte = np.frexp(amax)[1] - 1 + 127 - 7
    else:
        mant, ex = np.frexp(amax / 6.0)
        byte = np.where(mant > 0.5, ex, ex - 1) + 127
    byte = np.clip(np.where(amax > 0, byte, 1), 1, 254)
    scaled = (w * np.exp2(127.0 - byte)[:, None, :]).reshape(k, n).astype(np.float32)
    by_word = np.ascontiguousarray(scaled.reshape(k // 512, 128, 4, n).transpose(0, 1, 3, 2))
    if fmt == "e4m3":
        words = by_word.astype(ml_dtypes.float8_e4m3fn).view(np.uint8)
    else:
        c = by_word.astype(ml_dtypes.float4_e2m1fn).view(np.uint8) & 0xF
        words = (c[..., 0::2] | (c[..., 1::2] << 4)).reshape(k // 512, 128, 2 * n)
    return np.ascontiguousarray(words), np.ascontiguousarray(byte.astype(np.uint8).reshape(k // 512, 16, n))


def unpack_weight(words, scales, fmt):
    g, _, n = scales.shape
    words = np.ascontiguousarray(words).reshape(g, 128, n, -1)
    if fmt == "e4m3":
        vals = words.view(ml_dtypes.float8_e4m3fn).astype(np.float64)
    else:
        nib = np.empty((g, 128, n, 4), np.uint8)
        nib[..., 0::2] = words & 0xF
        nib[..., 1::2] = words >> 4
        vals = E2M1[nib]
    vals = vals * np.repeat(np.exp2(scales.astype(np.float64) - 127.0), 8, axis=1)[..., None]
    return vals.transpose(0, 1, 3, 2).reshape(g * 512, n)


D, E, T, I, Q = 512, 512, 2048, 512, 128


def setup_inputs():
    n = np.random.standard_normal
    idx = np.random.permutation(T)[:I]
    fd = mx_kscale(D)
    fe = mx_kscale(E)
    keysp = pack_weight(n((D, T)) / fd[:, None], "e4m3")
    valsp = pack_weight(n((E, T)) / fe[:, None], "e4m3")
    return {
        "query": (n((D, Q)) * 0.7 / np.sqrt(D) * fd[:, None]).astype(np.float32),
        "keys_words": keysp[0],
        "keys_scales": keysp[1],
        "gout": (n((E, Q)) * 1 / np.sqrt(E) * fe[:, None]).astype(np.float32),
        "vals_words": valsp[0],
        "vals_scales": valsp[1],
        "base": (0.5 * n((Q, I))).astype(np.float32),
        "offs": striped(idx),
    }


def reference(query, keys_words, keys_scales, gout, vals_words, vals_scales, base, offs):
    idx = unstriped(offs)
    keysu = unpack_weight(keys_words, keys_scales, "e4m3")
    valsu = unpack_weight(vals_words, vals_scales, "e4m3")
    queryq = mxq(f64(query), 0, "e4m3")
    keysidxg = keysu[:, idx]
    a = queryq.T @ keysidxg
    p = np.exp(a - np.max(a, axis=1, keepdims=True))
    n2 = np.sqrt(np.sum(np.square(p), axis=1, keepdims=True))
    goutq = mxq(f64(gout), 0, "e4m3")
    valsidxg = valsu[:, idx]
    c0 = goutq.T @ valsidxg
    dn2 = np.sum(c0 * p / np.square(n2) * (-1.0), axis=1, keepdims=True)
    dp = c0 / n2 + dn2 * 0.5 / np.sqrt(np.sum(np.square(p), axis=1, keepdims=True)) * p * 2.0
    da = dp * p
    hda = da * 16.0 * 2.0 * 16.0
    hdp = hda * p
    hdn2 = np.sum(hdp * 2.0 * p, axis=1, keepdims=True) / np.sqrt(np.sum(np.square(p), axis=1, keepdims=True)) * 0.5
    hn2 = np.sum(hdp * c0 / np.square(n2) * (-1.0), axis=1, keepdims=True) + np.sum(hdn2 * (-1.0) * c0 * p / np.square(np.square(n2)) * (-1.0), axis=1, keepdims=True) * n2 * 2.0
    hp = hda * dp + np.sum(hdp * 2.0 * p, axis=1, keepdims=True) * dn2 * 0.5 / np.square(np.sqrt(np.sum(np.square(p), axis=1, keepdims=True))) * (-1.0) * 0.5 / np.sqrt(np.sum(np.square(p), axis=1, keepdims=True)) * p * 2.0 + hdp * 2.0 * dn2 * 0.5 / np.sqrt(np.sum(np.square(p), axis=1, keepdims=True)) + hdn2 * (-1.0) / np.square(n2) * c0 + hn2 * 0.5 / np.sqrt(np.sum(np.square(p), axis=1, keepdims=True)) * p * 2.0
    ha = hp * p
    y = ha + f64(base)
    return y

@@ -1,0 +1,199 @@
+from contextlib import ExitStack
+
+import concourse.mybir as mybir
+
+D, E, T, I, Q = 512, 512, 2048, 512, 128
+FLOPS = 2 * Q * I * (D + E)
+
+F32 = mybir.dt.float32
+BF16 = mybir.dt.bfloat16
+I32 = mybir.dt.int32
+U32 = mybir.dt.uint32
+U16 = mybir.dt.uint16
+U8 = mybir.dt.uint8
+FP8X4 = mybir.dt.float8_e4m3fn_x4
+ALU = mybir.AluOpType
+ACT = mybir.ActivationFunctionType
+AX = mybir.AxisListType
+
+P = 128
+PACK = 4
+HALF = I // 2
+VAL_ROW = 4
+
+
+def tile_attend_gpunitweights_kernel(tc, query, keys_words, keys_scales, gout, vals_words, vals_scales, base, offs, out):
+    nc = tc.nc
+    halves = [slice(0, HALF), slice(HALF, I)]
+
+    with ExitStack() as ctx:
+        keep = ctx.enter_context(tc.tile_pool(name="keep", bufs=1))
+        reuse = ctx.enter_context(tc.tile_pool(name="reuse", bufs=1))
+        psum = ctx.enter_context(tc.psum_pool(name="psum", bufs=1))
+
+        offsets = keep.tile([P, I // 16], U16, name="offsets")
+        nc.sync.dma_start(offsets[:], offs)
+
+        k_bytes = reuse.tile([P, T], U8, name="k_bytes", align_bytes=64, offset=0)
+        v_bytes = reuse.tile([P, T], U8, name="v_bytes", align_bytes=64, offset=2048)
+        nc.vector.memset(k_bytes[:].bitcast(I32), 0)
+        nc.vector.memset(v_bytes[:].bitcast(I32), 0)
+        for quad in range(4):
+            nc.sync.dma_start(
+                out=k_bytes[32 * quad : 32 * quad + 4, :].bitcast(I32),
+                in_=keys_scales[0, 4 * quad : 4 * quad + 4, :].bitcast(I32),
+            )
+        for quad in range(4):
+            nc.gpsimd.dma_start(
+                out=v_bytes[32 * quad + VAL_ROW : 32 * quad + VAL_ROW + 4, :].bitcast(I32),
+                in_=vals_scales[0, 4 * quad : 4 * quad + 4, :].bitcast(I32),
+            )
+
+        q_raw = reuse.tile([P, PACK, Q], F32, name="q_raw", offset=12288)
+        nc.scalar.dma_start(out=q_raw[:], in_=query.rearrange("(p j) w -> p j w", j=PACK))
+        k_pool = reuse.tile([P, T], I32, name="k_pool", offset=4096)
+        nc.scalar.dma_start(out=k_pool[:], in_=keys_words[0].rearrange("p n t -> p (n t)").bitcast(I32))
+        g_raw = reuse.tile([P, PACK, Q], F32, name="g_raw", offset=20480)
+        nc.scalar.dma_start(out=g_raw[:], in_=gout.rearrange("(p j) w -> p j w", j=PACK))
+
+        consts = keep.tile([P, 4], F32, name="consts")
+        for col, value in enumerate((-1.5, 128.0, -128.0, 64.0)):
+            nc.vector.memset(consts[:, col : col + 1], value)
+
+        def interleave(raw, name):
+            grouped = keep.tile([P, Q, PACK], BF16, name=name, align_bytes=64)
+            nc.scalar.activation(out=grouped[:], in_=raw[:].rearrange("p j w -> p w j"), func=ACT.Copy)
+            return grouped
+
+        def quantise(grouped, name, offset):
+            codes = reuse.tile([P, Q], U32, name=name + "_codes", align_bytes=64, offset=offset)
+            plane = reuse.tile([P, Q], U8, name=name + "_plane", align_bytes=64, offset=offset + 4 * Q)
+            nc.vector.quantize_mx(
+                out=codes[:].bitcast(FP8X4), scales=plane[:], in_=grouped[:].rearrange("p w j -> p (w j)")
+            )
+            return codes, plane
+
+        q_grouped = interleave(q_raw, "q_grouped")
+        v_pool = reuse.tile([P, T], I32, name="v_pool", offset=12288)
+        nc.sync.dma_start(out=v_pool[:], in_=vals_words[0].rearrange("p n t -> p (n t)").bitcast(I32))
+        g_grouped = interleave(g_raw, "g_grouped")
+        base_sb = reuse.tile([P, I], F32, name="base_sb", offset=20480)
+        nc.sync.dma_start(out=base_sb[:], in_=base)
+
+        k_plane = keep.tile([P, I], U8, name="k_plane", align_bytes=64)
+        nc.vector.tensor_copy(out=k_plane[:], in_=k_bytes[:].indirect(offsets[:]))
+        q_codes, q_plane = quantise(q_grouped, "q", 22528)
+        k_codes = reuse.tile([P, I], U32, name="k_codes", align_bytes=64, offset=0)
+        nc.vector.tensor_copy(out=k_codes[:], in_=k_pool[:].bitcast(U32).indirect(offsets[:]))
+
+        a_ps = psum.tile([P, I], F32, name="a_ps")
+        nc.tensor.matmul_mx(
+            out=a_ps[:], lhsT=q_codes[:].bitcast(FP8X4), lhsT_scale=q_plane[:],
+            rhs=k_codes[:].bitcast(FP8X4), rhs_scale=k_plane[:], start=True, stop=True,
+        )
+
+        v_plane = reuse.tile([P, I], U8, name="v_plane", align_bytes=64, offset=4096)
+        nc.vector.tensor_copy(out=v_plane[:], in_=v_bytes[:].indirect(offsets[:]))
+        g_codes, g_plane = quantise(g_grouped, "g", 3072)
+
+        neg_max = keep.tile([P, 1], F32, name="neg_max")
+        nc.vector.tensor_reduce(out=neg_max[:], in_=a_ps[:], axis=AX.X, op=ALU.max, negate=True)
+        p = keep.tile([P, I], F32, name="p")
+        nc.scalar.activation(out=p[:], in_=a_ps[:], func=ACT.Exp, bias=neg_max[:], scale=1.0)
+        p2 = keep.tile([P, I], F32, name="p2")
+        s2 = keep.tile([P, 1], F32, name="s2")
+        nc.scalar.activation(out=p2[:], in_=p[:], func=ACT.Square, accum_out=s2[:])
+        p4 = keep.tile([P, I], F32, name="p4")
+        s4 = keep.tile([P, 1], F32, name="s4")
+        nc.scalar.activation(out=p4[:], in_=p2[:], func=ACT.Square, accum_out=s4[:])
+
+        c_ps = []
+        v_codes = reuse.tile([P, I], U32, name="v_codes", align_bytes=64, offset=1024)
+        for h, cols in enumerate(halves):
+            nc.vector.tensor_copy(
+                out=v_codes[:, cols],
+                in_=v_pool[:].bitcast(U32).indirect(offsets[:, h * HALF // 16 : (h + 1) * HALF // 16]),
+            )
+            bank = psum.tile([P, HALF], F32, name="c_ps%d" % h)
+            nc.tensor.matmul_mx(
+                out=bank[:], lhsT=g_codes[:].bitcast(FP8X4), lhsT_scale=g_plane[:],
+                rhs=v_codes[:, cols].bitcast(FP8X4), rhs_scale=v_plane[VAL_ROW:P, cols], start=True, stop=True,
+            )
+            c_ps.append(bank)
+
+        w = keep.tile([P, I], F32, name="w")
+        m_parts = keep.tile([P, 2], F32, name="m_parts")
+        nc.vector.scalar_tensor_tensor(
+            out=w[:, halves[0]], in0=c_ps[0][:], scalar=2.0 / 3.0, in1=p[:, halves[0]],
+            op0=ALU.mult, op1=ALU.mult, accum_out=m_parts[:, 0:1],
+        )
+        r = reuse.tile([P, 1], F32, name="r", offset=12288)
+        nc.vector.reciprocal(out=r[:], in_=s2[:])
+        nc.vector.scalar_tensor_tensor(
+            out=w[:, halves[1]], in0=c_ps[1][:], scalar=2.0 / 3.0, in1=p[:, halves[1]],
+            op0=ALU.mult, op1=ALU.mult, accum_out=m_parts[:, 1:2],
+        )
+        by_r = keep.tile([P, 4], F32, name="by_r")
+        nc.scalar.activation(out=by_r[:], in_=consts[:], func=ACT.Copy, scale=r[:])
+        by_r2 = keep.tile([P, 2], F32, name="by_r2")
+        nc.scalar.activation(out=by_r2[:], in_=by_r[:, 2:4], func=ACT.Copy, scale=r[:])
+        kappa4 = by_r[:, 1:2]
+
+        n_parts = keep.tile([P, 3], F32, name="n_parts")
+        wp = keep.tile([P, I], F32, name="wp")
+        for h, cols in enumerate(halves):
+            nc.vector.scalar_tensor_tensor(
+                out=wp[:, cols], in0=w[:, cols], scalar=1.5, in1=p2[:, cols],
+                op0=ALU.mult, op1=ALU.mult, accum_out=n_parts[:, h : h + 1],
+            )
+        neg_lam = keep.tile([P, 1], F32, name="neg_lam")
+        m_terms = keep.tile([P, 2], F32, name="m_terms")
+        nc.scalar.activation(out=m_terms[:], in_=m_parts[:], func=ACT.Copy, scale=by_r[:, 0:1], accum_out=neg_lam[:])
+        nc.scalar.activation(out=n_parts[:, 2:3], in_=s4[:], func=ACT.Copy, scale=neg_lam[:])
+        alpha = keep.tile([P, 1], F32, name="alpha")
+        n_terms = keep.tile([P, 3], F32, name="n_terms")
+        nc.scalar.activation(out=n_terms[:], in_=n_parts[:], func=ACT.Copy, scale=r[:], accum_out=alpha[:])
+
+        z = keep.tile([P, I], F32, name="z")
+        nc.vector.scalar_tensor_tensor(out=z[:], in0=p2[:], scalar=neg_lam[:], in1=w[:], op0=ALU.mult, op1=ALU.add)
+
+        low = keep.tile([P, I], F32, name="low")
+        low_sums = keep.tile([P, 2], F32, name="low_sums")
+        for h, cols in enumerate(halves):
+            nc.scalar.activation(
+                out=low[:, cols], in_=p2[:, cols], func=ACT.Square, scale=neg_lam[:], bias=alpha[:],
+                accum_out=low_sums[:, h : h + 1],
+            )
+        high = keep.tile([P, I], F32, name="high")
+        high_sums = keep.tile([P, 2], F32, name="high_sums")
+        for h, cols in enumerate(halves):
+            nc.scalar.activation(
+                out=high[:, cols], in_=z[:, cols], func=ACT.Square, scale=-3.0, bias=alpha[:],
+                accum_out=high_sums[:, h : h + 1],
+            )
+        low_half = keep.tile([P, 1], F32, name="low_half")
+        low_terms = keep.tile([P, 2], F32, name="low_terms")
+        nc.scalar.activation(out=low_terms[:], in_=low_sums[:], func=ACT.Copy, scale=by_r2[:, 1:2], accum_out=low_half[:])
+        coef = keep.tile([P, 1], F32, name="coef")
+        coef_terms = keep.tile([P, 2], F32, name="coef_terms")
+        nc.scalar.activation(
+            out=coef_terms[:], in_=high_sums[:], func=ACT.Identity, scale=by_r2[:, 0:1], bias=low_half[:],
+            accum_out=coef[:],
+        )
+
+        less = keep.tile([P, I], F32, name="less")
+        for cols in halves:
+            nc.vector.scalar_tensor_tensor(
+                out=less[:, cols], in0=low[:, cols], scalar=kappa4, in1=base_sb[:, cols], op0=ALU.mult, op1=ALU.subtract
+            )
+        most = keep.tile([P, I], F32, name="most")
+        for cols in halves:
+            nc.vector.scalar_tensor_tensor(
+                out=most[:, cols], in0=high[:, cols], scalar=kappa4, in1=less[:, cols], op0=ALU.mult, op1=ALU.subtract
+            )
+        result = keep.tile([P, I], F32, name="result")
+        for cols in halves:
+            nc.vector.scalar_tensor_tensor(
+                out=result[:, cols], in0=p2[:, cols], scalar=coef[:], in1=most[:, cols], op0=ALU.mult, op1=ALU.add
+            )
+            nc.sync.dma_start(out=out[:, cols], in_=result[:, cols])

@@ -20,6 +20,7 @@ P = 128
 PACK = 4
 HALF = I // 2
 VAL_ROW = 4
+EARLY = T // 4
 
 
 def tile_attend_gpunitweights_kernel(tc, query, keys_words, keys_scales, gout, vals_words, vals_scales, base, offs, out):
@@ -38,23 +39,28 @@ def tile_attend_gpunitweights_kernel(tc, query, keys_words, keys_scales, gout, v
         v_bytes = reuse.tile([P, T], U8, name="v_bytes", align_bytes=64, offset=2048)
         nc.vector.memset(k_bytes[:].bitcast(I32), 0)
         nc.vector.memset(v_bytes[:].bitcast(I32), 0)
-        for quad in range(4):
-            nc.sync.dma_start(
-                out=k_bytes[32 * quad : 32 * quad + 4, :].bitcast(I32),
-                in_=keys_scales[0, 4 * quad : 4 * quad + 4, :].bitcast(I32),
-            )
-        for quad in range(4):
-            nc.gpsimd.dma_start(
-                out=v_bytes[32 * quad + VAL_ROW : 32 * quad + VAL_ROW + 4, :].bitcast(I32),
-                in_=vals_scales[0, 4 * quad : 4 * quad + 4, :].bitcast(I32),
-            )
 
-        q_raw = reuse.tile([P, PACK, Q], F32, name="q_raw", offset=12288)
-        nc.scalar.dma_start(out=q_raw[:], in_=query.rearrange("(p j) w -> p j w", j=PACK))
+        def load_scale_rows(window, rows, first):
+            for quad in range(4):
+                nc.sync.dma_start(
+                    out=window[32 * quad + first : 32 * quad + first + 4, :].bitcast(I32),
+                    in_=rows[0, 4 * quad : 4 * quad + 4, :].bitcast(I32),
+                )
+
+        q_raw = keep.tile([P, PACK, Q], F32, name="q_raw")
+        nc.sync.dma_start(out=q_raw[:], in_=query.rearrange("(p j) w -> p j w", j=PACK))
         k_pool = reuse.tile([P, T], I32, name="k_pool", offset=4096)
-        nc.scalar.dma_start(out=k_pool[:], in_=keys_words[0].rearrange("p n t -> p (n t)").bitcast(I32))
-        g_raw = reuse.tile([P, PACK, Q], F32, name="g_raw", offset=20480)
-        nc.scalar.dma_start(out=g_raw[:], in_=gout.rearrange("(p j) w -> p j w", j=PACK))
+        k_words = keys_words[0].rearrange("p n t -> p (n t)").bitcast(I32)
+        nc.sync.dma_start(out=k_pool[:, :EARLY], in_=k_words[:, :EARLY])
+        load_scale_rows(k_bytes, keys_scales, 0)
+        nc.sync.dma_start(out=k_pool[:, EARLY:], in_=k_words[:, EARLY:])
+        g_raw = keep.tile([P, PACK, Q], F32, name="g_raw")
+        nc.sync.dma_start(out=g_raw[:], in_=gout.rearrange("(p j) w -> p j w", j=PACK))
+        load_scale_rows(v_bytes, vals_scales, VAL_ROW)
+        v_pool = reuse.tile([P, T], I32, name="v_pool", offset=12288)
+        nc.sync.dma_start(out=v_pool[:], in_=vals_words[0].rearrange("p n t -> p (n t)").bitcast(I32))
+        base_sb = keep.tile([P, I], F32, name="base_sb")
+        nc.sync.dma_start(out=base_sb[:], in_=base)
 
         consts = keep.tile([P, 4], F32, name="consts")
         for col, value in enumerate((-1.5, 128.0, -128.0, 64.0)):
@@ -74,11 +80,7 @@ def tile_attend_gpunitweights_kernel(tc, query, keys_words, keys_scales, gout, v
             return codes, plane
 
         q_grouped = interleave(q_raw, "q_grouped")
-        v_pool = reuse.tile([P, T], I32, name="v_pool", offset=12288)
-        nc.sync.dma_start(out=v_pool[:], in_=vals_words[0].rearrange("p n t -> p (n t)").bitcast(I32))
         g_grouped = interleave(g_raw, "g_grouped")
-        base_sb = reuse.tile([P, I], F32, name="base_sb", offset=20480)
-        nc.sync.dma_start(out=base_sb[:], in_=base)
 
         k_plane = keep.tile([P, I], U8, name="k_plane", align_bytes=64)
         nc.vector.tensor_copy(out=k_plane[:], in_=k_bytes[:].indirect(offsets[:]))
@@ -94,9 +96,9 @@ def tile_attend_gpunitweights_kernel(tc, query, keys_words, keys_scales, gout, v
 
         v_plane = reuse.tile([P, I], U8, name="v_plane", align_bytes=64, offset=4096)
         nc.vector.tensor_copy(out=v_plane[:], in_=v_bytes[:].indirect(offsets[:]))
-        g_codes, g_plane = quantise(g_grouped, "g", 3072)
+        g_codes, g_plane = quantise(g_grouped, "g", 23552)
 
-        neg_max = keep.tile([P, 1], F32, name="neg_max")
+        neg_max = reuse.tile([P, 1], F32, name="neg_max", offset=3072)
         nc.vector.tensor_reduce(out=neg_max[:], in_=a_ps[:], axis=AX.X, op=ALU.max, negate=True)
         p = keep.tile([P, I], F32, name="p")
         nc.scalar.activation(out=p[:], in_=a_ps[:], func=ACT.Exp, bias=neg_max[:], scale=1.0)

from contextlib import ExitStack

import concourse.mybir as mybir

D, E, T, I, Q = 512, 512, 2048, 512, 128
FLOPS = 2 * Q * I * (D + E)

F32 = mybir.dt.float32
BF16 = mybir.dt.bfloat16
I32 = mybir.dt.int32
U32 = mybir.dt.uint32
U16 = mybir.dt.uint16
U8 = mybir.dt.uint8
FP8X4 = mybir.dt.float8_e4m3fn_x4
ALU = mybir.AluOpType
ACT = mybir.ActivationFunctionType
AX = mybir.AxisListType

P = 128
PACK = 4
HALF = I // 2
VAL_ROW = 4
EARLY = T // 4


def tile_attend_gpunitweights_kernel(tc, query, keys_words, keys_scales, gout, vals_words, vals_scales, base, offs, out):
    nc = tc.nc
    halves = [slice(0, HALF), slice(HALF, I)]

    with ExitStack() as ctx:
        keep = ctx.enter_context(tc.tile_pool(name="keep", bufs=1))
        reuse = ctx.enter_context(tc.tile_pool(name="reuse", bufs=1))
        psum = ctx.enter_context(tc.psum_pool(name="psum", bufs=1))

        offsets = keep.tile([P, I // 16], U16, name="offsets")
        nc.sync.dma_start(offsets[:], offs)

        k_bytes = reuse.tile([P, T], U8, name="k_bytes", align_bytes=64, offset=0)
        v_bytes = reuse.tile([P, T], U8, name="v_bytes", align_bytes=64, offset=2048)
        nc.vector.memset(k_bytes[:].bitcast(I32), 0)
        nc.vector.memset(v_bytes[:].bitcast(I32), 0)

        def load_scale_rows(window, rows, first):
            for quad in range(4):
                nc.sync.dma_start(
                    out=window[32 * quad + first : 32 * quad + first + 4, :].bitcast(I32),
                    in_=rows[0, 4 * quad : 4 * quad + 4, :].bitcast(I32),
                )

        q_raw = keep.tile([P, PACK, Q], F32, name="q_raw")
        nc.sync.dma_start(out=q_raw[:], in_=query.rearrange("(p j) w -> p j w", j=PACK))
        k_pool = reuse.tile([P, T], I32, name="k_pool", offset=4096)
        k_words = keys_words[0].rearrange("p n t -> p (n t)").bitcast(I32)
        nc.sync.dma_start(out=k_pool[:, :EARLY], in_=k_words[:, :EARLY])
        load_scale_rows(k_bytes, keys_scales, 0)
        nc.sync.dma_start(out=k_pool[:, EARLY:], in_=k_words[:, EARLY:])
        g_raw = keep.tile([P, PACK, Q], F32, name="g_raw")
        nc.sync.dma_start(out=g_raw[:], in_=gout.rearrange("(p j) w -> p j w", j=PACK))
        load_scale_rows(v_bytes, vals_scales, VAL_ROW)
        v_pool = reuse.tile([P, T], I32, name="v_pool", offset=12288)
        nc.sync.dma_start(out=v_pool[:], in_=vals_words[0].rearrange("p n t -> p (n t)").bitcast(I32))
        base_sb = keep.tile([P, I], F32, name="base_sb")
        nc.sync.dma_start(out=base_sb[:], in_=base)

        consts = keep.tile([P, 4], F32, name="consts")
        for col, value in enumerate((-1.5, 128.0, -128.0, 64.0)):
            nc.vector.memset(consts[:, col : col + 1], value)

        def interleave(raw, name):
            grouped = keep.tile([P, Q, PACK], BF16, name=name, align_bytes=64)
            nc.scalar.activation(out=grouped[:], in_=raw[:].rearrange("p j w -> p w j"), func=ACT.Copy)
            return grouped

        def quantise(grouped, name, offset):
            codes = reuse.tile([P, Q], U32, name=name + "_codes", align_bytes=64, offset=offset)
            plane = reuse.tile([P, Q], U8, name=name + "_plane", align_bytes=64, offset=offset + 4 * Q)
            nc.vector.quantize_mx(
                out=codes[:].bitcast(FP8X4), scales=plane[:], in_=grouped[:].rearrange("p w j -> p (w j)")
            )
            return codes, plane

        q_grouped = interleave(q_raw, "q_grouped")
        g_grouped = interleave(g_raw, "g_grouped")

        k_plane = keep.tile([P, I], U8, name="k_plane", align_bytes=64)
        nc.vector.tensor_copy(out=k_plane[:], in_=k_bytes[:].indirect(offsets[:]))
        q_codes, q_plane = quantise(q_grouped, "q", 22528)
        k_codes = reuse.tile([P, I], U32, name="k_codes", align_bytes=64, offset=0)
        nc.vector.tensor_copy(out=k_codes[:], in_=k_pool[:].bitcast(U32).indirect(offsets[:]))

        a_ps = psum.tile([P, I], F32, name="a_ps")
        nc.tensor.matmul_mx(
            out=a_ps[:], lhsT=q_codes[:].bitcast(FP8X4), lhsT_scale=q_plane[:],
            rhs=k_codes[:].bitcast(FP8X4), rhs_scale=k_plane[:], start=True, stop=True,
        )

        v_plane = reuse.tile([P, I], U8, name="v_plane", align_bytes=64, offset=4096)
        nc.vector.tensor_copy(out=v_plane[:], in_=v_bytes[:].indirect(offsets[:]))
        g_codes, g_plane = quantise(g_grouped, "g", 23552)

        neg_max = reuse.tile([P, 1], F32, name="neg_max", offset=3072)
        nc.vector.tensor_reduce(out=neg_max[:], in_=a_ps[:], axis=AX.X, op=ALU.max, negate=True)
        p = keep.tile([P, I], F32, name="p")
        nc.scalar.activation(out=p[:], in_=a_ps[:], func=ACT.Exp, bias=neg_max[:], scale=1.0)
        p2 = keep.tile([P, I], F32, name="p2")
        s2 = keep.tile([P, 1], F32, name="s2")
        nc.scalar.activation(out=p2[:], in_=p[:], func=ACT.Square, accum_out=s2[:])
        p4 = keep.tile([P, I], F32, name="p4")
        s4 = keep.tile([P, 1], F32, name="s4")
        nc.scalar.activation(out=p4[:], in_=p2[:], func=ACT.Square, accum_out=s4[:])

        c_ps = []
        v_codes = reuse.tile([P, I], U32, name="v_codes", align_bytes=64, offset=1024)
        for h, cols in enumerate(halves):
            nc.vector.tensor_copy(
                out=v_codes[:, cols],
                in_=v_pool[:].bitcast(U32).indirect(offsets[:, h * HALF // 16 : (h + 1) * HALF // 16]),
            )
            bank = psum.tile([P, HALF], F32, name="c_ps%d" % h)
            nc.tensor.matmul_mx(
                out=bank[:], lhsT=g_codes[:].bitcast(FP8X4), lhsT_scale=g_plane[:],
                rhs=v_codes[:, cols].bitcast(FP8X4), rhs_scale=v_plane[VAL_ROW:P, cols], start=True, stop=True,
            )
            c_ps.append(bank)

        w = keep.tile([P, I], F32, name="w")
        m_parts = keep.tile([P, 2], F32, name="m_parts")
        nc.vector.scalar_tensor_tensor(
            out=w[:, halves[0]], in0=c_ps[0][:], scalar=2.0 / 3.0, in1=p[:, halves[0]],
            op0=ALU.mult, op1=ALU.mult, accum_out=m_parts[:, 0:1],
        )
        r = reuse.tile([P, 1], F32, name="r", offset=12288)
        nc.vector.reciprocal(out=r[:], in_=s2[:])
        nc.vector.scalar_tensor_tensor(
            out=w[:, halves[1]], in0=c_ps[1][:], scalar=2.0 / 3.0, in1=p[:, halves[1]],
            op0=ALU.mult, op1=ALU.mult, accum_out=m_parts[:, 1:2],
        )
        by_r = keep.tile([P, 4], F32, name="by_r")
        nc.scalar.activation(out=by_r[:], in_=consts[:], func=ACT.Copy, scale=r[:])
        by_r2 = keep.tile([P, 2], F32, name="by_r2")
        nc.scalar.activation(out=by_r2[:], in_=by_r[:, 2:4], func=ACT.Copy, scale=r[:])
        kappa4 = by_r[:, 1:2]

        n_parts = keep.tile([P, 3], F32, name="n_parts")
        wp = keep.tile([P, I], F32, name="wp")
        for h, cols in enumerate(halves):
            nc.vector.scalar_tensor_tensor(
                out=wp[:, cols], in0=w[:, cols], scalar=1.5, in1=p2[:, cols],
                op0=ALU.mult, op1=ALU.mult, accum_out=n_parts[:, h : h + 1],
            )
        neg_lam = keep.tile([P, 1], F32, name="neg_lam")
        m_terms = keep.tile([P, 2], F32, name="m_terms")
        nc.scalar.activation(out=m_terms[:], in_=m_parts[:], func=ACT.Copy, scale=by_r[:, 0:1], accum_out=neg_lam[:])
        nc.scalar.activation(out=n_parts[:, 2:3], in_=s4[:], func=ACT.Copy, scale=neg_lam[:])
        alpha = keep.tile([P, 1], F32, name="alpha")
        n_terms = keep.tile([P, 3], F32, name="n_terms")
        nc.scalar.activation(out=n_terms[:], in_=n_parts[:], func=ACT.Copy, scale=r[:], accum_out=alpha[:])

        z = keep.tile([P, I], F32, name="z")
        nc.vector.scalar_tensor_tensor(out=z[:], in0=p2[:], scalar=neg_lam[:], in1=w[:], op0=ALU.mult, op1=ALU.add)

        low = keep.tile([P, I], F32, name="low")
        low_sums = keep.tile([P, 2], F32, name="low_sums")
        for h, cols in enumerate(halves):
            nc.scalar.activation(
                out=low[:, cols], in_=p2[:, cols], func=ACT.Square, scale=neg_lam[:], bias=alpha[:],
                accum_out=low_sums[:, h : h + 1],
            )
        high = keep.tile([P, I], F32, name="high")
        high_sums = keep.tile([P, 2], F32, name="high_sums")
        for h, cols in enumerate(halves):
            nc.scalar.activation(
                out=high[:, cols], in_=z[:, cols], func=ACT.Square, scale=-3.0, bias=alpha[:],
                accum_out=high_sums[:, h : h + 1],
            )
        low_half = keep.tile([P, 1], F32, name="low_half")
        low_terms = keep.tile([P, 2], F32, name="low_terms")
        nc.scalar.activation(out=low_terms[:], in_=low_sums[:], func=ACT.Copy, scale=by_r2[:, 1:2], accum_out=low_half[:])
        coef = keep.tile([P, 1], F32, name="coef")
        coef_terms = keep.tile([P, 2], F32, name="coef_terms")
        nc.scalar.activation(
            out=coef_terms[:], in_=high_sums[:], func=ACT.Identity, scale=by_r2[:, 0:1], bias=low_half[:],
            accum_out=coef[:],
        )

        less = keep.tile([P, I], F32, name="less")
        for cols in halves:
            nc.vector.scalar_tensor_tensor(
                out=less[:, cols], in0=low[:, cols], scalar=kappa4, in1=base_sb[:, cols], op0=ALU.mult, op1=ALU.subtract
            )
        most = keep.tile([P, I], F32, name="most")
        for cols in halves:
            nc.vector.scalar_tensor_tensor(
                out=most[:, cols], in0=high[:, cols], scalar=kappa4, in1=less[:, cols], op0=ALU.mult, op1=ALU.subtract
            )
        result = keep.tile([P, I], F32, name="result")
        for cols in halves:
            nc.vector.scalar_tensor_tensor(
                out=result[:, cols], in0=p2[:, cols], scalar=coef[:], in1=most[:, cols], op0=ALU.mult, op1=ALU.add
            )
            nc.sync.dma_start(out=out[:, cols], in_=result[:, cols])
